import numpy as np
import ml_dtypes


def mxq(x, axis, fmt="e4m3"):
    dtype, down = {"e4m3": (ml_dtypes.float8_e4m3fn, 7), "e5m2": (ml_dtypes.float8_e5m2, 14)}[fmt]
    v = np.moveaxis(np.asarray(x, np.float32).astype(ml_dtypes.bfloat16).astype(np.float64), axis, -1)
    blocks = v.reshape(v.shape[:-1] + (-1, 32))
    amax = np.abs(blocks).max(-1, keepdims=True)
    byte = np.maximum(np.where(amax > 0, np.frexp(amax)[1] - 1 + 127, 0) - down, 1)
    scale = np.exp2(byte - 127.0)
    codes = (blocks / scale).astype(np.float32).astype(dtype).astype(np.float64)
    return np.moveaxis((codes * scale).reshape(v.shape), -1, axis)


WIDE = False


def mx_kscale(k):
    if not WIDE:
        return np.ones(k)
    levels = np.array([10, -10, 5, -5, 0])
    if k % 512:
        return np.exp2(np.random.permutation(np.resize(levels, k // 32))).repeat(32)
    a = np.empty((k // 512, 16))
    for p in range(k // 512):
        a[p, :8] = np.random.permutation(np.resize(levels, 8))
        for g in range(8):
            far = levels[np.abs(levels - a[p, g]) >= 10]
            a[p, g + 8] = far[np.random.randint(len(far))]
    return np.exp2(a.ravel()).repeat(32)


def f64(x):
    return np.asarray(x).astype(np.float64)


def striped(idx):
    return np.tile(idx.reshape(-1, 16).T, (8, 1)).astype(np.uint16)


def unstriped(offs):
    return offs[:16].T.reshape(-1).astype(np.int64)


def silu(v):
    return v / (1.0 + np.exp(-np.maximum(v, -700.0)))


K, T, E, C, H, N = 1024, 768, 2, 256, 512, 256


def by_expert(wq, xq):
    return np.concatenate([wq[e].T @ xq[:, e * C:(e + 1) * C] for e in range(E)], axis=1)


def setup_inputs():
    n = np.random.standard_normal
    s = mx_kscale(K)[:, None]
    u = mx_kscale(H)
    return {
        "xT": (n((K, T)) * s).astype(np.float32),
        "w1": (n((E + 1, K, H)) / np.sqrt(K) / s[None]).astype(np.float32),
        "w3": (n((E + 1, K, H)) / np.sqrt(K) / s[None] * u[None, None, :]).astype(np.float32),
        "w2": (n((E + 1, H, N)) / np.sqrt(H) / u[None, :, None]).astype(np.float32),
        "gate": np.tile(np.random.uniform(0.2, 1.0, E * C), (N, 1)).astype(np.float32),
        "offs": striped(np.random.permutation(T)[:E * C]),
    }


def reference(xT, w1, w3, w2, gate, offs):
    idx = unstriped(offs)
    w1q, w3q, w2q = mxq(f64(w1), 1, "e4m3"), mxq(f64(w3), 1, "e4m3"), mxq(f64(w2), 1, "e4m3")
    xs = mxq(f64(xT), 0, "e4m3")
    hs = silu(w1q[E].T @ xs) * (w3q[E].T @ xs)
    ys = w2q[E].T @ mxq(hs, 0, "e4m3")
    xq = mxq(f64(xT)[:, idx], 0, "e4m3")
    h = silu(by_expert(w1q, xq))
    h = h * by_expert(w3q, xq)
    y = by_expert(w2q, mxq(h, 0, "e4m3"))
    out = ys
    out[:, idx] += f64(gate) * y
    return out

@@ -1,0 +1,238 @@
+from contextlib import ExitStack
+
+import concourse.mybir as mybir
+
+K, T, E, C, H, N = 1024, 768, 2, 256, 512, 256
+FLOPS = 2 * (E * C + T) * (2 * K * H + H * N)
+
+F32 = mybir.dt.float32
+BF16 = mybir.dt.bfloat16
+U32 = mybir.dt.uint32
+U16 = mybir.dt.uint16
+U8 = mybir.dt.uint8
+FP8X4 = mybir.dt.float8_e4m3fn_x4
+MULT = mybir.AluOpType.mult
+ADD = mybir.AluOpType.add
+SILU = mybir.ActivationFunctionType.Silu
+
+P = 128
+J = 4
+PASSES = K // (P * J)
+TOK = 128
+SHARED = E
+
+
+def tile_moe_shr_glu_silu_kernel(tc, xT, w1, w3, w2, gate, offs, out):
+    nc = tc.nc
+    with ExitStack() as ctx:
+        keep = ctx.enter_context(tc.tile_pool(name="keep", bufs=1))
+        xraw = ctx.enter_context(tc.tile_pool(name="xraw", bufs=2))
+        wraw = ctx.enter_context(tc.tile_pool(name="wraw", bufs=8))
+        vraw = ctx.enter_context(tc.tile_pool(name="vraw", bufs=3))
+        group = ctx.enter_context(tc.tile_pool(name="group", bufs=4))
+        work = ctx.enter_context(tc.tile_pool(name="work", bufs=3))
+        psum = ctx.enter_context(tc.psum_pool(name="psum", bufs=2))
+        psum1 = ctx.enter_context(tc.psum_pool(name="psum1", bufs=1))
+
+        offsets = keep.tile([P, E * C // 16], U16, name="offsets")
+        gates = keep.tile([P, E * C], F32, name="gates")
+
+        warm = keep.tile([P, 8], F32, name="warm")
+        nc.vector.memset(warm[:], 0.0)
+        warm2 = keep.tile([P, 8], F32, name="warm2")
+        nc.scalar.activation(warm2[:], warm[:], SILU)
+        routed = [keep.tile([P, T], F32, name=f"routed{r}") for r in range(2)]
+        for r in range(2):
+            nc.gpsimd.memset(routed[r][:], 0.0)
+
+        x_raw = []
+        for s in range(PASSES):
+            xr = xraw.tile([P, J, T], F32, name="xr")
+            view = xT[s * 512 : (s + 1) * 512, :].rearrange("(p j) t -> p j t", j=J)
+            for c in range(0, T, 384):
+                nc.sync.dma_start(xr[:, :, c : c + 384], view[:, :, c : c + 384])
+            x_raw.append(xr)
+        nc.sync.dma_start(offsets[:], offs)
+
+        def codes_of(width, name):
+            c = keep.tile([P, width], U32, name=name + "_codes", align_bytes=64)
+            z = keep.tile([P, width], U8, name=name + "_scales", align_bytes=64)
+            return c, z
+
+        def quantize(dst, c0, src, width):
+            nc.vector.quantize_mx(
+                out=dst[0][:, c0 : c0 + width].bitcast(FP8X4), scales=dst[1][:, c0 : c0 + width], in_=src
+            )
+
+        def mm(acc, lhs, m0, rhs, n0, n, start, stop):
+            nc.tensor.matmul_mx(
+                out=acc,
+                lhsT=lhs[0][:, m0 : m0 + P].bitcast(FP8X4),
+                lhsT_scale=lhs[1][:, m0 : m0 + P],
+                rhs=rhs[0][:, n0 : n0 + n].bitcast(FP8X4),
+                rhs_scale=rhs[1][:, n0 : n0 + n],
+                start=start,
+                stop=stop,
+            )
+
+        copiers = {"S": nc.scalar.copy, "V": nc.vector.tensor_copy, "G": nc.gpsimd.tensor_copy}
+
+        def cast_plain(copy, dst, src, i=4):
+            copy(dst.rearrange("p (c i) j -> p c j i", i=i), src.rearrange("p j (c i) -> p c j i", i=i))
+
+        xs = [codes_of(T, f"xs{s}") for s in range(PASSES)]
+        xg = [codes_of(E * C, f"xg{s}") for s in range(PASSES)]
+        PAIR = ["V","V","V","V","V","V","V","V"]
+        X4 = ["S","S","S","S"]
+        V2 = {"v0":"S","v1":"S","vs":"S"}
+        ACT = {"w1s":[320,320],"w3s":[320,320],"w1e":[320,320],"w3e":[320,320],"w1f":[320,320],"w3f":[320,320]}
+
+        def tokens(s):
+            xr = x_raw[s]
+            pairs = [keep.tile([P, T, 2], BF16, name=f"pairs{s}{h}") for h in range(2)]
+            x4 = group.tile([P, T, J], BF16, name="x4", bufs=2, align_bytes=64)
+            for k, c in enumerate(range(0, T, 384)):
+                for h in range(2):
+                    cast_plain(copiers[PAIR[s * 4 + k * 2 + h]], pairs[h][:, c : c + 384, :], xr[:, 2 * h : 2 * h + 2, c : c + 384])
+                cast_plain(copiers[X4[s * 2 + k]], x4[:, c : c + 384, :], xr[:, :, c : c + 384])
+            g4 = group.tile([P, E * C * J], BF16, name="g4", bufs=2, align_bytes=64)
+            words = g4[:].bitcast(U32).rearrange("p (n h) -> p n h", h=2)
+            for h in range(2):
+                window = pairs[h][:].rearrange("p t e -> p (t e)").bitcast(U32)
+                nc.vector.tensor_copy(words[:, :, h], window.indirect(offsets[:]))
+            x4f = x4[:].rearrange("p t j -> p (t j)")
+            quantize(xs[s], 0, x4f[:, :2048], 512)
+            quantize(xs[s], 512, x4f[:, 2048:], 256)
+            quantize(xg[s], 0, g4[:], 512)
+
+        done = {}
+        order = {"w1s": (w1, SHARED), "w3s": (w3, SHARED), "w1e": (w1, 0), "w3e": (w3, 0), "w1f": (w1, 1), "w3f": (w3, 1)}
+
+        def cast_w(g, wr, lo, hi, act):
+            dst = g[:].rearrange("p (t m j) -> p m j t", t=J, j=J)
+            src = wr[:].rearrange("p j (m t) -> p m j t", t=J)
+            lo, hi, cut = lo // J, hi // J, (lo + act) // J
+            if cut > lo:
+                nc.scalar.copy(dst[:, lo:cut], src[:, lo:cut])
+            if cut < hi:
+                nc.vector.tensor_copy(dst[:, cut:hi], src[:, cut:hi])
+
+        def weights(name, s, parts):
+            w, e = order[name]
+            wr = wraw.tile([P, J, H], F32, name="wr")
+            view = w[e, s * 512 : (s + 1) * 512, :].rearrange("(p j) c -> p j c", j=J)
+            step = H // parts
+            g = group.tile([P, J * H], BF16, name="g", align_bytes=64)
+            for c in range(0, H, step):
+                nc.sync.dma_start(wr[:, :, c : c + step], view[:, :, c : c + step])
+                cast_w(g, wr, c, c + step, ACT[name][s] // parts)
+            c = codes_of(H, f"{name}{s}")
+            quantize(c, 0, g[:], H)
+            done.setdefault(name, []).append(c)
+
+        def weights2(name, e):
+            vr = vraw.tile([P, J, N], F32, name="vr")
+            nc.sync.dma_start(vr[:], w2[e].rearrange("(p j) c -> p j c", j=J))
+            c = codes_of(N, name)
+            g = group.tile([P, N, J], BF16, name="gv", bufs=2, align_bytes=64)
+            cast_plain(copiers[V2[name]], g[:], vr[:])
+            quantize(c, 0, g[:].rearrange("p n j -> p (n j)"), N)
+            done[name] = c
+
+        def product(wc, x, col, name):
+            acc = psum.tile([P, J, TOK], F32, name=name)
+            for t in range(J):
+                for s in range(PASSES):
+                    mm(acc[:, t, :], wc[s], t * P, x[s], col, TOK, s == 0, s == PASSES - 1)
+            return acc
+
+        silus = {}
+
+        def front(key, w1c, x, col):
+            a = product(w1c, x, col, "a")
+            sl = work.tile([P, TOK, J], F32, name="sl", bufs=6)
+            nc.scalar.activation(sl[:], a[:].rearrange("p t n -> p n t"), SILU)
+            silus[key] = sl
+
+        def back(key, w3c, x, col, hc, hcol):
+            b = product(w3c, x, col, "b")
+            h = work.tile([P, TOK, J], BF16, name="h", align_bytes=64)
+            nc.vector.tensor_tensor(h[:], b[:].rearrange("p t n -> p n t"), silus[key][:], MULT)
+            quantize(hc, hcol, h[:].rearrange("p n t -> p (n t)"), TOK)
+
+        hs = codes_of(T, "hs")
+        he = [codes_of(C, f"he{e}") for e in range(E)]
+        ys = [psum1.tile([P, 2, C], F32, name=f"ys{i}") for i in range(3)]
+
+        def results(e, v):
+            y = psum1.tile([P, 2, C], F32, name="y")
+            for r in range(2):
+                mm(y[:, r, :], v, r * P, he[e], 0, C, True, True)
+                yr = work.tile([P, C], F32, name="yr")
+                nc.scalar.copy(yr[:], y[:, r, :])
+                nc.vector.tensor_tensor(
+                    routed[r][:].indirect(offsets[:, e * C // 16 : (e + 1) * C // 16]),
+                    yr[:], gates[:, e * C : (e + 1) * C], MULT,
+                )
+
+        def shared_sum(c):
+            for r in range(2):
+                mm(ys[c][:, r, :], done["vs"], r * P, hs, c * C, C, True, True)
+
+        def store(c, halves):
+            for r in range(2):
+                o = work.tile([P, C], F32, name="o", bufs=3)
+                nc.vector.tensor_tensor(o[:], ys[c][:, r, :], routed[r][:, c * C : (c + 1) * C], ADD)
+                nc.sync.dma_start(out[r * P : (r + 1) * P, c * C : (c + 1) * C], o[:])
+
+        def store_rows():
+            for r in range(2):
+                o = work.tile([P, T], F32, name="o", bufs=2)
+                for c in range(3):
+                    nc.vector.tensor_tensor(o[:, c * C : (c + 1) * C], ys[c][:, r, :], routed[r][:, c * C : (c + 1) * C], ADD)
+                nc.sync.dma_start(out[r * P : (r + 1) * P, :], o[:])
+
+        tokens(0)
+        tokens(1)
+        weights("w1s", 0, 1)
+        weights("w1s", 1, 1)
+        weights("w3s", 0, 1)
+        front(("s", 0), done["w1s"], xs, 0 * TOK)
+        front(("s", 1), done["w1s"], xs, 1 * TOK)
+        weights("w3s", 1, 1)
+        front(("s", 2), done["w1s"], xs, 2 * TOK)
+        front(("s", 3), done["w1s"], xs, 3 * TOK)
+        weights("w1e", 0, 1)
+        front(("s", 4), done["w1s"], xs, 4 * TOK)
+        front(("s", 5), done["w1s"], xs, 5 * TOK)
+        back(("s", 0), done["w3s"], xs, 0 * TOK, hs, 0 * TOK)
+        back(("s", 1), done["w3s"], xs, 1 * TOK, hs, 1 * TOK)
+        weights("w1e", 1, 1)
+        back(("s", 2), done["w3s"], xs, 2 * TOK, hs, 2 * TOK)
+        back(("s", 3), done["w3s"], xs, 3 * TOK, hs, 3 * TOK)
+        weights("w3e", 0, 1)
+        front((0, 0), done["w1e"], xg, 0 * C + 0 * TOK)
+        front((0, 1), done["w1e"], xg, 0 * C + 1 * TOK)
+        back(("s", 4), done["w3s"], xs, 4 * TOK, hs, 4 * TOK)
+        back(("s", 5), done["w3s"], xs, 5 * TOK, hs, 5 * TOK)
+        weights("w3e", 1, 1)
+        weights2("v0", 0)
+        nc.sync.dma_start(gates[:], gate[0:P, :])
+        weights("w1f", 0, 1)
+        back((0, 0), done["w3e"], xg, 0 * C + 0 * TOK, he[0], 0 * TOK)
+        back((0, 1), done["w3e"], xg, 0 * C + 1 * TOK, he[0], 1 * TOK)
+        weights("w1f", 1, 1)
+        results(0, done["v0"])
+        weights("w3f", 0, 1)
+        front((1, 0), done["w1f"], xg, 1 * C + 0 * TOK)
+        front((1, 1), done["w1f"], xg, 1 * C + 1 * TOK)
+        weights("w3f", 1, 2)
+        weights2("v1", 1)
+        weights2("vs", SHARED)
+        back((1, 0), done["w3f"], xg, 1 * C + 0 * TOK, he[1], 0 * TOK)
+        back((1, 1), done["w3f"], xg, 1 * C + 1 * TOK, he[1], 1 * TOK)
+        shared_sum(0)
+        shared_sum(1)
+        shared_sum(2)
+        results(1, done["v1"])
+        store_rows()

@@ -27,7 +27,7 @@ def tile_moe_shr_glu_silu_kernel(tc, xT, w1, w3, w2, gate, offs, out):
     with ExitStack() as ctx:
         keep = ctx.enter_context(tc.tile_pool(name="keep", bufs=1))
         xraw = ctx.enter_context(tc.tile_pool(name="xraw", bufs=2))
-        wraw = ctx.enter_context(tc.tile_pool(name="wraw", bufs=8))
+        wraw = ctx.enter_context(tc.tile_pool(name="wraw", bufs=7))
         vraw = ctx.enter_context(tc.tile_pool(name="vraw", bufs=3))
         group = ctx.enter_context(tc.tile_pool(name="group", bufs=4))
         work = ctx.enter_context(tc.tile_pool(name="work", bufs=3))
@@ -75,17 +75,20 @@ def tile_moe_shr_glu_silu_kernel(tc, xT, w1, w3, w2, gate, offs, out):
                 stop=stop,
             )
 
-        copiers = {"S": nc.scalar.copy, "V": nc.vector.tensor_copy, "G": nc.gpsimd.tensor_copy}
+        def gps_copy(out, in_):
+            nc.gpsimd.tensor_scalar(out, in_, 1.0, 0.0, MULT, ADD)
+
+        copiers = {"S": nc.scalar.copy, "V": nc.vector.tensor_copy, "G": gps_copy}
 
         def cast_plain(copy, dst, src, i=4):
             copy(dst.rearrange("p (c i) j -> p c j i", i=i), src.rearrange("p j (c i) -> p c j i", i=i))
 
         xs = [codes_of(T, f"xs{s}") for s in range(PASSES)]
         xg = [codes_of(E * C, f"xg{s}") for s in range(PASSES)]
-        PAIR = ["V","V","V","V","V","V","V","V"]
-        X4 = ["S","S","S","S"]
+        PAIR = ["S","V","V","S","V","S","V","S"]
+        X4 = ["V","V","S","S"]
         V2 = {"v0":"S","v1":"S","vs":"S"}
-        ACT = {"w1s":[320,320],"w3s":[320,320],"w1e":[320,320],"w3e":[320,320],"w1f":[320,320],"w3f":[320,320]}
+        WHO = {"w1s":["S","S"],"w3s":["V","SV"],"w1e":["SV","S"],"w3e":["S","V"],"w1f":["S","SV"],"w3f":["S",["S","V"]]}
 
         def tokens(s):
             xr = x_raw[s]
@@ -108,14 +111,13 @@ def tile_moe_shr_glu_silu_kernel(tc, xT, w1, w3, w2, gate, offs, out):
         done = {}
         order = {"w1s": (w1, SHARED), "w3s": (w3, SHARED), "w1e": (w1, 0), "w3e": (w3, 0), "w1f": (w1, 1), "w3f": (w3, 1)}
 
-        def cast_w(g, wr, lo, hi, act):
+        def cast_w(g, wr, lo, hi, who):
             dst = g[:].rearrange("p (t m j) -> p m j t", t=J, j=J)
             src = wr[:].rearrange("p j (m t) -> p m j t", t=J)
-            lo, hi, cut = lo // J, hi // J, (lo + act) // J
-            if cut > lo:
-                nc.scalar.copy(dst[:, lo:cut], src[:, lo:cut])
-            if cut < hi:
-                nc.vector.tensor_copy(dst[:, cut:hi], src[:, cut:hi])
+            step = (hi - lo) // J // len(who)
+            for i, w in enumerate(who):
+                a = lo // J + i * step
+                copiers[w](dst[:, a : a + step], src[:, a : a + step])
 
         def weights(name, s, parts):
             w, e = order[name]
@@ -125,7 +127,7 @@ def tile_moe_shr_glu_silu_kernel(tc, xT, w1, w3, w2, gate, offs, out):
             g = group.tile([P, J * H], BF16, name="g", align_bytes=64)
             for c in range(0, H, step):
                 nc.sync.dma_start(wr[:, :, c : c + step], view[:, :, c : c + step])
-                cast_w(g, wr, c, c + step, ACT[name][s] // parts)
+                cast_w(g, wr, c, c + step, WHO[name][s] if parts == 1 else WHO[name][s][c // step])
             c = codes_of(H, f"{name}{s}")
             quantize(c, 0, g[:], H)
             done.setdefault(name, []).append(c)
@@ -154,11 +156,18 @@ def tile_moe_shr_glu_silu_kernel(tc, xT, w1, w3, w2, gate, offs, out):
             nc.scalar.activation(sl[:], a[:].rearrange("p t n -> p n t"), SILU)
             silus[key] = sl
 
+        pending = []
+
         def back(key, w3c, x, col, hc, hcol):
             b = product(w3c, x, col, "b")
-            h = work.tile([P, TOK, J], BF16, name="h", align_bytes=64)
-            nc.vector.tensor_tensor(h[:], b[:].rearrange("p t n -> p n t"), silus[key][:], MULT)
-            quantize(hc, hcol, h[:].rearrange("p n t -> p (n t)"), TOK)
+            if not pending:
+                h2 = work.tile([P, 2, TOK, J], BF16, name="h2", align_bytes=64)
+                pending.append(h2)
+                nc.vector.tensor_tensor(h2[:, 0], b[:].rearrange("p t n -> p n t"), silus[key][:], MULT)
+            else:
+                h2 = pending.pop()
+                nc.vector.tensor_tensor(h2[:, 1], b[:].rearrange("p t n -> p n t"), silus[key][:], MULT)
+                quantize(hc, hcol - TOK, h2[:].rearrange("p c n t -> p (c n t)"), 2 * TOK)
 
         hs = codes_of(T, "hs")
         he = [codes_of(C, f"he{e}") for e in range(E)]
@@ -166,40 +175,36 @@ def tile_moe_shr_glu_silu_kernel(tc, xT, w1, w3, w2, gate, offs, out):
 
         def results(e, v):
             y = psum1.tile([P, 2, C], F32, name="y")
+            yr = work.tile([P, 2, C], F32, name="yr", bufs=2)
+            cols = slice(e * C, (e + 1) * C)
             for r in range(2):
                 mm(y[:, r, :], v, r * P, he[e], 0, C, True, True)
-                yr = work.tile([P, C], F32, name="yr")
-                nc.scalar.copy(yr[:], y[:, r, :])
-                nc.vector.tensor_tensor(
-                    routed[r][:].indirect(offsets[:, e * C // 16 : (e + 1) * C // 16]),
-                    yr[:], gates[:, e * C : (e + 1) * C], MULT,
-                )
-
-        def shared_sum(c):
             for r in range(2):
-                mm(ys[c][:, r, :], done["vs"], r * P, hs, c * C, C, True, True)
-
-        def store(c, halves):
+                nc.vector.tensor_tensor(yr[:, r, :], y[:, r, :], gates[:, cols], MULT)
             for r in range(2):
-                o = work.tile([P, C], F32, name="o", bufs=3)
-                nc.vector.tensor_tensor(o[:], ys[c][:, r, :], routed[r][:, c * C : (c + 1) * C], ADD)
-                nc.sync.dma_start(out[r * P : (r + 1) * P, c * C : (c + 1) * C], o[:])
+                nc.vector.tensor_copy(routed[r][:].indirect(offsets[:, e * C // 16 : (e + 1) * C // 16]), yr[:, r, :])
+
+        def shared_sum():
+            for r in range(2):
+                mm(ys[r][:].rearrange("p a c -> p (a c)"), done["vs"], r * P, hs, 0, 512, True, True)
+            for r in range(2):
+                mm(ys[2][:, r, :], done["vs"], r * P, hs, 512, C, True, True)
 
         def store_rows():
             for r in range(2):
                 o = work.tile([P, T], F32, name="o", bufs=2)
-                for c in range(3):
-                    nc.vector.tensor_tensor(o[:, c * C : (c + 1) * C], ys[c][:, r, :], routed[r][:, c * C : (c + 1) * C], ADD)
+                nc.vector.tensor_tensor(o[:, :512], ys[r][:].rearrange("p a c -> p (a c)"), routed[r][:, :512], ADD)
+                nc.vector.tensor_tensor(o[:, 512:], ys[2][:, r, :], routed[r][:, 512:], ADD)
                 nc.sync.dma_start(out[r * P : (r + 1) * P, :], o[:])
 
         tokens(0)
-        tokens(1)
         weights("w1s", 0, 1)
         weights("w1s", 1, 1)
+        tokens(1)
         weights("w3s", 0, 1)
+        weights("w3s", 1, 1)
         front(("s", 0), done["w1s"], xs, 0 * TOK)
         front(("s", 1), done["w1s"], xs, 1 * TOK)
-        weights("w3s", 1, 1)
         front(("s", 2), done["w1s"], xs, 2 * TOK)
         front(("s", 3), done["w1s"], xs, 3 * TOK)
         weights("w1e", 0, 1)
@@ -210,14 +215,14 @@ def tile_moe_shr_glu_silu_kernel(tc, xT, w1, w3, w2, gate, offs, out):
         weights("w1e", 1, 1)
         back(("s", 2), done["w3s"], xs, 2 * TOK, hs, 2 * TOK)
         back(("s", 3), done["w3s"], xs, 3 * TOK, hs, 3 * TOK)
-        weights("w3e", 0, 1)
         front((0, 0), done["w1e"], xg, 0 * C + 0 * TOK)
         front((0, 1), done["w1e"], xg, 0 * C + 1 * TOK)
+        weights("w3e", 0, 1)
+        nc.sync.dma_start(gates[:], gate[0:P, :])
+        weights2("v0", 0)
+        weights("w3e", 1, 1)
         back(("s", 4), done["w3s"], xs, 4 * TOK, hs, 4 * TOK)
         back(("s", 5), done["w3s"], xs, 5 * TOK, hs, 5 * TOK)
-        weights("w3e", 1, 1)
-        weights2("v0", 0)
-        nc.sync.dma_start(gates[:], gate[0:P, :])
         weights("w1f", 0, 1)
         back((0, 0), done["w3e"], xg, 0 * C + 0 * TOK, he[0], 0 * TOK)
         back((0, 1), done["w3e"], xg, 0 * C + 1 * TOK, he[0], 1 * TOK)
@@ -228,11 +233,9 @@ def tile_moe_shr_glu_silu_kernel(tc, xT, w1, w3, w2, gate, offs, out):
         front((1, 1), done["w1f"], xg, 1 * C + 1 * TOK)
         weights("w3f", 1, 2)
         weights2("v1", 1)
-        weights2("vs", SHARED)
+        weights2("vs", 2)
         back((1, 0), done["w3f"], xg, 1 * C + 0 * TOK, he[1], 0 * TOK)
         back((1, 1), done["w3f"], xg, 1 * C + 1 * TOK, he[1], 1 * TOK)
-        shared_sum(0)
-        shared_sum(1)
-        shared_sum(2)
+        shared_sum()
         results(1, done["v1"])
         store_rows()

@@ -19,14 +19,14 @@ P = 128
 J = 4
 PASSES = K // (P * J)
 TOK = 128
-SHARED = E
+XT = 384
 
 
 def tile_moe_shr_glu_silu_kernel(tc, xT, w1, w3, w2, gate, offs, out):
     nc = tc.nc
     with ExitStack() as ctx:
         keep = ctx.enter_context(tc.tile_pool(name="keep", bufs=1))
-        xraw = ctx.enter_context(tc.tile_pool(name="xraw", bufs=2))
+        xraw = ctx.enter_context(tc.tile_pool(name="xraw", bufs=1))
         wraw = ctx.enter_context(tc.tile_pool(name="wraw", bufs=7))
         vraw = ctx.enter_context(tc.tile_pool(name="vraw", bufs=3))
         group = ctx.enter_context(tc.tile_pool(name="group", bufs=4))
@@ -45,14 +45,10 @@ def tile_moe_shr_glu_silu_kernel(tc, xT, w1, w3, w2, gate, offs, out):
         for r in range(2):
             nc.gpsimd.memset(routed[r][:], 0.0)
 
-        x_raw = []
-        for s in range(PASSES):
-            xr = xraw.tile([P, J, T], F32, name="xr")
-            view = xT[s * 512 : (s + 1) * 512, :].rearrange("(p j) t -> p j t", j=J)
-            for c in range(0, T, 384):
-                nc.sync.dma_start(xr[:, :, c : c + 384], view[:, :, c : c + 384])
-            x_raw.append(xr)
-        nc.sync.dma_start(offsets[:], offs)
+        def gps_copy(out, in_):
+            nc.gpsimd.tensor_scalar(out, in_, 1.0, 0.0, MULT, ADD)
+
+        copiers = {"S": nc.scalar.copy, "V": nc.vector.tensor_copy, "G": gps_copy}
 
         def codes_of(width, name):
             c = keep.tile([P, width], U32, name=name + "_codes", align_bytes=64)
@@ -75,167 +71,256 @@ def tile_moe_shr_glu_silu_kernel(tc, xT, w1, w3, w2, gate, offs, out):
                 stop=stop,
             )
 
-        def gps_copy(out, in_):
-            nc.gpsimd.tensor_scalar(out, in_, 1.0, 0.0, MULT, ADD)
-
-        copiers = {"S": nc.scalar.copy, "V": nc.vector.tensor_copy, "G": gps_copy}
-
         def cast_plain(copy, dst, src, i=4):
             copy(dst.rearrange("p (c i) j -> p c j i", i=i), src.rearrange("p j (c i) -> p c j i", i=i))
 
+        EXPERT = {"e": 0, "f": 1, "s": E}
+        MATRIX = {"1": w1, "3": w3}
+
+        x_raw = [xraw.tile([P, J, T], F32, name=f"xr{s}") for s in range(PASSES)]
+        w_raw = {}
+        v_raw = {}
+        codes = {}
+        pairs = [[keep.tile([P, T, 2], BF16, name=f"pairs{s}{h}") for h in range(2)] for s in range(PASSES)]
+        x4 = [group.tile([P, T, J], BF16, name=f"x4{s}", bufs=1, align_bytes=64) for s in range(PASSES)]
+        g4 = [group.tile([P, E * C * J], BF16, name=f"g4{s}", bufs=1, align_bytes=64) for s in range(PASSES)]
         xs = [codes_of(T, f"xs{s}") for s in range(PASSES)]
         xg = [codes_of(E * C, f"xg{s}") for s in range(PASSES)]
-        PAIR = ["S","V","V","S","V","S","V","S"]
-        X4 = ["V","V","S","S"]
-        V2 = {"v0":"S","v1":"S","vs":"S"}
-        WHO = {"w1s":["S","S"],"w3s":["V","SV"],"w1e":["SV","S"],"w3e":["S","V"],"w1f":["S","SV"],"w3f":["S",["S","V"]]}
+        hidden = {"s": codes_of(T, "hs"), "e": codes_of(C, "he"), "f": codes_of(C, "hf")}
 
-        def tokens(s):
-            xr = x_raw[s]
-            pairs = [keep.tile([P, T, 2], BF16, name=f"pairs{s}{h}") for h in range(2)]
-            x4 = group.tile([P, T, J], BF16, name="x4", bufs=2, align_bytes=64)
-            for k, c in enumerate(range(0, T, 384)):
-                for h in range(2):
-                    cast_plain(copiers[PAIR[s * 4 + k * 2 + h]], pairs[h][:, c : c + 384, :], xr[:, 2 * h : 2 * h + 2, c : c + 384])
-                cast_plain(copiers[X4[s * 2 + k]], x4[:, c : c + 384, :], xr[:, :, c : c + 384])
-            g4 = group.tile([P, E * C * J], BF16, name="g4", bufs=2, align_bytes=64)
-            words = g4[:].bitcast(U32).rearrange("p (n h) -> p n h", h=2)
-            for h in range(2):
-                window = pairs[h][:].rearrange("p t e -> p (t e)").bitcast(U32)
-                nc.vector.tensor_copy(words[:, :, h], window.indirect(offsets[:]))
-            x4f = x4[:].rearrange("p t j -> p (t j)")
-            quantize(xs[s], 0, x4f[:, :2048], 512)
-            quantize(xs[s], 512, x4f[:, 2048:], 256)
-            quantize(xg[s], 0, g4[:], 512)
+        def load_x(s, h):
+            view = xT[s * 512 : (s + 1) * 512, :].rearrange("(p j) t -> p j t", j=J)
+            nc.sync.dma_start(x_raw[s][:, 2 * h : 2 * h + 2, :], view[:, 2 * h : 2 * h + 2, :])
 
-        done = {}
-        order = {"w1s": (w1, SHARED), "w3s": (w3, SHARED), "w1e": (w1, 0), "w3e": (w3, 0), "w1f": (w1, 1), "w3f": (w3, 1)}
-
-        def cast_w(g, wr, lo, hi, who):
-            dst = g[:].rearrange("p (t m j) -> p m j t", t=J, j=J)
-            src = wr[:].rearrange("p j (m t) -> p m j t", t=J)
-            step = (hi - lo) // J // len(who)
-            for i, w in enumerate(who):
-                a = lo // J + i * step
-                copiers[w](dst[:, a : a + step], src[:, a : a + step])
-
-        def weights(name, s, parts):
-            w, e = order[name]
+        def load_w(name, parts):
+            w, e, s = MATRIX[name[1]], EXPERT[name[2]], int(name[3])
             wr = wraw.tile([P, J, H], F32, name="wr")
             view = w[e, s * 512 : (s + 1) * 512, :].rearrange("(p j) c -> p j c", j=J)
             step = H // parts
-            g = group.tile([P, J * H], BF16, name="g", align_bytes=64)
             for c in range(0, H, step):
                 nc.sync.dma_start(wr[:, :, c : c + step], view[:, :, c : c + step])
-                cast_w(g, wr, c, c + step, WHO[name][s] if parts == 1 else WHO[name][s][c // step])
-            c = codes_of(H, f"{name}{s}")
-            quantize(c, 0, g[:], H)
-            done.setdefault(name, []).append(c)
+            w_raw[name] = wr
 
-        def weights2(name, e):
+        def load_v(name):
             vr = vraw.tile([P, J, N], F32, name="vr")
-            nc.sync.dma_start(vr[:], w2[e].rearrange("(p j) c -> p j c", j=J))
-            c = codes_of(N, name)
-            g = group.tile([P, N, J], BF16, name="gv", bufs=2, align_bytes=64)
-            cast_plain(copiers[V2[name]], g[:], vr[:])
-            quantize(c, 0, g[:].rearrange("p n j -> p (n j)"), N)
-            done[name] = c
+            nc.sync.dma_start(vr[:], w2[{"v0": 0, "v1": 1, "vs": E}[name]].rearrange("(p j) c -> p j c", j=J))
+            v_raw[name] = vr
 
-        def product(wc, x, col, name):
+        def cast_pair(s, h, c, who):
+            cast_plain(copiers[who], pairs[s][h][:], x_raw[s][:, 2 * h : 2 * h + 2, :])
+
+        def cast_x(s, c, who):
+            cast_plain(copiers[who], x4[s][:, c * XT : (c + 1) * XT, :], x_raw[s][:, :, c * XT : (c + 1) * XT])
+
+        def gather(s, h):
+            words = g4[s][:].bitcast(U32).rearrange("p (n h) -> p n h", h=2)
+            window = pairs[s][h][:].rearrange("p t e -> p (t e)").bitcast(U32)
+            nc.vector.tensor_copy(words[:, :, h], window.indirect(offsets[:]))
+
+        def quantize_x(s):
+            x4f = x4[s][:].rearrange("p t j -> p (t j)")
+            quantize(xs[s], 0, x4f[:, :2048], 512)
+            quantize(xs[s], 512, x4f[:, 2048:], 256)
+
+        def quantize_g(s):
+            quantize(xg[s], 0, g4[s][:], 512)
+
+        grouped = {}
+
+        def cast_w(name, who):
+            g = group.tile([P, J * H], BF16, name="g", align_bytes=64)
+            grouped[name] = g
+            dst = g[:].rearrange("p (t m j) -> p m j t", t=J, j=J)
+            src = w_raw[name][:].rearrange("p j (m t) -> p m j t", t=J)
+            step = P // len(who)
+            a = 0
+            for w in sorted(set(who)):
+                b = a + who.count(w) * step
+                copiers[w](dst[:, a:b], src[:, a:b])
+                a = b
+
+        def quantize_w(name):
+            codes[name] = codes_of(H, name)
+            quantize(codes[name], 0, grouped[name][:], H)
+
+        def cast_v(name, who):
+            g = group.tile([P, N, J], BF16, name="gv", bufs=2, align_bytes=64)
+            grouped[name] = g
+            cast_plain(copiers[who], g[:], v_raw[name][:])
+
+        def quantize_v(name):
+            codes[name] = codes_of(N, name)
+            quantize(codes[name], 0, grouped[name][:].rearrange("p n j -> p (n j)"), N)
+
+        def product(w, e, i, name):
+            x, col = (xs, i * TOK) if e == "s" else (xg, EXPERT[e] * C + i * TOK)
             acc = psum.tile([P, J, TOK], F32, name=name)
             for t in range(J):
                 for s in range(PASSES):
-                    mm(acc[:, t, :], wc[s], t * P, x[s], col, TOK, s == 0, s == PASSES - 1)
+                    mm(acc[:, t, :], codes[f"{w}{e}{s}"], t * P, x[s], col, TOK, s == 0, s == PASSES - 1)
             return acc
 
         silus = {}
+        h2 = {}
 
-        def front(key, w1c, x, col):
-            a = product(w1c, x, col, "a")
+        def front(e, i):
+            a = product("w1", e, i, "a")
             sl = work.tile([P, TOK, J], F32, name="sl", bufs=6)
             nc.scalar.activation(sl[:], a[:].rearrange("p t n -> p n t"), SILU)
-            silus[key] = sl
+            silus[e, i] = sl
 
-        pending = []
-
-        def back(key, w3c, x, col, hc, hcol):
-            b = product(w3c, x, col, "b")
-            if not pending:
-                h2 = work.tile([P, 2, TOK, J], BF16, name="h2", align_bytes=64)
-                pending.append(h2)
-                nc.vector.tensor_tensor(h2[:, 0], b[:].rearrange("p t n -> p n t"), silus[key][:], MULT)
+        def back(e, i, who="V"):
+            b = product("w3", e, i, "b")
+            if (e, i // 2) not in h2:
+                hh = work.tile([P, 2, TOK, J], BF16, name="hh", align_bytes=64)
+                h2[e, i // 2] = hh
+            dst = h2[e, i // 2][:, i % 2]
+            if who == "G":
+                bc = work.tile([P, TOK, J], F32, name="bc", bufs=2)
+                nc.scalar.copy(bc[:], b[:].rearrange("p t n -> p n t"))
+                nc.gpsimd.tensor_tensor(dst, bc[:], silus[e, i][:], MULT)
             else:
-                h2 = pending.pop()
-                nc.vector.tensor_tensor(h2[:, 1], b[:].rearrange("p t n -> p n t"), silus[key][:], MULT)
-                quantize(hc, hcol - TOK, h2[:].rearrange("p c n t -> p (c n t)"), 2 * TOK)
+                nc.vector.tensor_tensor(dst, b[:].rearrange("p t n -> p n t"), silus[e, i][:], MULT)
 
-        hs = codes_of(T, "hs")
-        he = [codes_of(C, f"he{e}") for e in range(E)]
+        def quantize_h(e, k):
+            quantize(hidden[e], k * 2 * TOK, h2[e, k][:].rearrange("p c n t -> p (c n t)"), 2 * TOK)
+
         ys = [psum1.tile([P, 2, C], F32, name=f"ys{i}") for i in range(3)]
+        weighted = {}
 
-        def results(e, v):
+        def result(e):
             y = psum1.tile([P, 2, C], F32, name="y")
             yr = work.tile([P, 2, C], F32, name="yr", bufs=2)
-            cols = slice(e * C, (e + 1) * C)
             for r in range(2):
-                mm(y[:, r, :], v, r * P, he[e], 0, C, True, True)
-            for r in range(2):
-                nc.vector.tensor_tensor(yr[:, r, :], y[:, r, :], gates[:, cols], MULT)
-            for r in range(2):
-                nc.vector.tensor_copy(routed[r][:].indirect(offsets[:, e * C // 16 : (e + 1) * C // 16]), yr[:, r, :])
+                mm(y[:, r, :], codes[{"e": "v0", "f": "v1"}[e]], r * P, hidden[e], 0, C, True, True)
+            gate_e = gates[:, EXPERT[e] * C : (EXPERT[e] + 1) * C].rearrange("p (o c) -> p o c", o=1).to_broadcast([P, 2, C])
+            nc.vector.tensor_tensor(yr[:], y[:], gate_e, MULT)
+            weighted[e] = yr
+
+        def scatter(e, r):
+            cols = offsets[:, EXPERT[e] * C // 16 : (EXPERT[e] + 1) * C // 16]
+            nc.vector.tensor_copy(routed[r][:].indirect(cols), weighted[e][:, r, :])
 
         def shared_sum():
             for r in range(2):
-                mm(ys[r][:].rearrange("p a c -> p (a c)"), done["vs"], r * P, hs, 0, 512, True, True)
+                mm(ys[r][:].rearrange("p a c -> p (a c)"), codes["vs"], r * P, hidden["s"], 0, 512, True, True)
             for r in range(2):
-                mm(ys[2][:, r, :], done["vs"], r * P, hs, 512, C, True, True)
+                mm(ys[2][:, r, :], codes["vs"], r * P, hidden["s"], 512, C, True, True)
 
-        def store_rows():
-            for r in range(2):
-                o = work.tile([P, T], F32, name="o", bufs=2)
+        ysum = work.tile([P, T], F32, name="ysum", bufs=1)
+
+        def shared_copy():
+            nc.scalar.copy(ysum[:, :512], ys[0][:].rearrange("p a c -> p (a c)"))
+            nc.scalar.copy(ysum[:, 512:], ys[2][:, 0, :])
+
+        def finish(r, who):
+            o = work.tile([P, T], F32, name="o", bufs=2)
+            if who == "G":
+                nc.gpsimd.tensor_tensor(o[:], routed[r][:], ysum[:], ADD)
+            else:
                 nc.vector.tensor_tensor(o[:, :512], ys[r][:].rearrange("p a c -> p (a c)"), routed[r][:, :512], ADD)
                 nc.vector.tensor_tensor(o[:, 512:], ys[2][:, r, :], routed[r][:, 512:], ADD)
-                nc.sync.dma_start(out[r * P : (r + 1) * P, :], o[:])
+            nc.sync.dma_start(out[r * P : (r + 1) * P, :], o[:])
 
-        tokens(0)
-        weights("w1s", 0, 1)
-        weights("w1s", 1, 1)
-        tokens(1)
-        weights("w3s", 0, 1)
-        weights("w3s", 1, 1)
-        front(("s", 0), done["w1s"], xs, 0 * TOK)
-        front(("s", 1), done["w1s"], xs, 1 * TOK)
-        front(("s", 2), done["w1s"], xs, 2 * TOK)
-        front(("s", 3), done["w1s"], xs, 3 * TOK)
-        weights("w1e", 0, 1)
-        front(("s", 4), done["w1s"], xs, 4 * TOK)
-        front(("s", 5), done["w1s"], xs, 5 * TOK)
-        back(("s", 0), done["w3s"], xs, 0 * TOK, hs, 0 * TOK)
-        back(("s", 1), done["w3s"], xs, 1 * TOK, hs, 1 * TOK)
-        weights("w1e", 1, 1)
-        back(("s", 2), done["w3s"], xs, 2 * TOK, hs, 2 * TOK)
-        back(("s", 3), done["w3s"], xs, 3 * TOK, hs, 3 * TOK)
-        front((0, 0), done["w1e"], xg, 0 * C + 0 * TOK)
-        front((0, 1), done["w1e"], xg, 0 * C + 1 * TOK)
-        weights("w3e", 0, 1)
+        nc.sync.dma_start(offsets[:], offs)
+        load_x(0, 0)
+        load_x(1, 0)
+        load_x(1, 1)
+        load_x(0, 1)
+        load_w("w1s1", 1)
+        load_w("w1s0", 1)
+        load_w("w3s1", 1)
+        load_w("w3s0", 1)
+        load_w("w1e0", 1)
+        load_w("w1e1", 1)
+        load_w("w1f1", 1)
+        load_w("w3e1", 1)
+        load_v("v0")
+        load_w("w3e0", 1)
+        load_w("w1f0", 1)
+        load_w("w3f0", 1)
+        load_w("w3f1", 2)
         nc.sync.dma_start(gates[:], gate[0:P, :])
-        weights2("v0", 0)
-        weights("w3e", 1, 1)
-        back(("s", 4), done["w3s"], xs, 4 * TOK, hs, 4 * TOK)
-        back(("s", 5), done["w3s"], xs, 5 * TOK, hs, 5 * TOK)
-        weights("w1f", 0, 1)
-        back((0, 0), done["w3e"], xg, 0 * C + 0 * TOK, he[0], 0 * TOK)
-        back((0, 1), done["w3e"], xg, 0 * C + 1 * TOK, he[0], 1 * TOK)
-        weights("w1f", 1, 1)
-        results(0, done["v0"])
-        weights("w3f", 0, 1)
-        front((1, 0), done["w1f"], xg, 1 * C + 0 * TOK)
-        front((1, 1), done["w1f"], xg, 1 * C + 1 * TOK)
-        weights("w3f", 1, 2)
-        weights2("v1", 1)
-        weights2("vs", 2)
-        back((1, 0), done["w3f"], xg, 1 * C + 0 * TOK, he[1], 0 * TOK)
-        back((1, 1), done["w3f"], xg, 1 * C + 1 * TOK, he[1], 1 * TOK)
+        load_v("vs")
+        load_v("v1")
+        cast_x(1, 0, "V")
+        cast_pair(0, 1, 0, "V")
+        cast_w("w1s1", "V")
+        gather(0, 1)
+        cast_pair(0, 0, 0, "V")
+        cast_x(0, 0, "S")
+        cast_w("w1s0", "S")
+        cast_pair(1, 0, 0, "S")
+        cast_x(0, 1, "S")
+        quantize_w("w1s0")
+        gather(1, 0)
+        gather(0, 0)
+        quantize_g(0)
+        quantize_x(0)
+        cast_w("w3s1", "S")
+        quantize_w("w1s1")
+        cast_x(1, 1, "S")
+        cast_pair(1, 1, 0, "G")
+        cast_w("w3s0", "V")
+        quantize_x(1)
+        cast_w("w1e0", "V")
+        front("s", 1)
+        cast_v("v0", "G")
+        quantize_w("w3s1")
+        gather(1, 1)
+        front("s", 2)
+        front("s", 0)
+        quantize_w("w3s0")
+        front("s", 5)
+        back("s", 1)
+        cast_w("w3e1", "SV")
+        front("s", 4)
+        quantize_g(1)
+        quantize_w("w1e0")
+        back("s", 5)
+        back("s", 0)
+        cast_w("w3e0", "V")
+        cast_w("w1e1", "S")
+        quantize_w("w3e1")
+        back("s", 2)
+        front("s", 3)
+        quantize_w("w1e1")
+        back("s", 4)
+        quantize_h("s", 0)
+        quantize_v("v0")
+        cast_w("w1f1", "V")
+        quantize_w("w3e0")
+        cast_w("w1f0", "S")
+        front("e", 0)
+        back("s", 3)
+        quantize_h("s", 2)
+        back("e", 0)
+        quantize_w("w1f1")
+        quantize_h("s", 1)
+        front("e", 1)
+        back("e", 1)
+        cast_w("w3f1", "S")
+        cast_w("w3f0", "S")
+        quantize_h("e", 0)
+        quantize_w("w3f1")
+        result("e")
+        quantize_w("w1f0")
+        quantize_w("w3f0")
+        scatter("e", 0)
+        front("f", 1)
+        front("f", 0)
+        back("f", 1)
+        back("f", 0)
+        cast_v("v1", "S")
+        cast_v("vs", "S")
+        quantize_v("v1")
+        quantize_h("f", 0)
+        quantize_v("vs")
+        scatter("e", 1)
         shared_sum()
-        results(1, done["v1"])
-        store_rows()
+        shared_copy()
+        result("f")
+        scatter("f", 0)
+        finish(0, "G")
+        scatter("f", 1)
+        finish(1, "V")

from contextlib import ExitStack

import concourse.mybir as mybir

K, T, E, C, H, N = 1024, 768, 2, 256, 512, 256
FLOPS = 2 * (E * C + T) * (2 * K * H + H * N)

F32 = mybir.dt.float32
BF16 = mybir.dt.bfloat16
U32 = mybir.dt.uint32
U16 = mybir.dt.uint16
U8 = mybir.dt.uint8
FP8X4 = mybir.dt.float8_e4m3fn_x4
MULT = mybir.AluOpType.mult
ADD = mybir.AluOpType.add
SILU = mybir.ActivationFunctionType.Silu

P = 128
J = 4
PASSES = K // (P * J)
TOK = 128
XT = 384


def tile_moe_shr_glu_silu_kernel(tc, xT, w1, w3, w2, gate, offs, out):
    nc = tc.nc
    with ExitStack() as ctx:
        keep = ctx.enter_context(tc.tile_pool(name="keep", bufs=1))
        xraw = ctx.enter_context(tc.tile_pool(name="xraw", bufs=1))
        wraw = ctx.enter_context(tc.tile_pool(name="wraw", bufs=7))
        vraw = ctx.enter_context(tc.tile_pool(name="vraw", bufs=3))
        group = ctx.enter_context(tc.tile_pool(name="group", bufs=4))
        work = ctx.enter_context(tc.tile_pool(name="work", bufs=3))
        psum = ctx.enter_context(tc.psum_pool(name="psum", bufs=2))
        psum1 = ctx.enter_context(tc.psum_pool(name="psum1", bufs=1))

        offsets = keep.tile([P, E * C // 16], U16, name="offsets")
        gates = keep.tile([P, E * C], F32, name="gates")

        warm = keep.tile([P, 8], F32, name="warm")
        nc.vector.memset(warm[:], 0.0)
        warm2 = keep.tile([P, 8], F32, name="warm2")
        nc.scalar.activation(warm2[:], warm[:], SILU)
        routed = [keep.tile([P, T], F32, name=f"routed{r}") for r in range(2)]
        for r in range(2):
            nc.gpsimd.memset(routed[r][:], 0.0)

        def gps_copy(out, in_):
            nc.gpsimd.tensor_scalar(out, in_, 1.0, 0.0, MULT, ADD)

        copiers = {"S": nc.scalar.copy, "V": nc.vector.tensor_copy, "G": gps_copy}

        def codes_of(width, name):
            c = keep.tile([P, width], U32, name=name + "_codes", align_bytes=64)
            z = keep.tile([P, width], U8, name=name + "_scales", align_bytes=64)
            return c, z

        def quantize(dst, c0, src, width):
            nc.vector.quantize_mx(
                out=dst[0][:, c0 : c0 + width].bitcast(FP8X4), scales=dst[1][:, c0 : c0 + width], in_=src
            )

        def mm(acc, lhs, m0, rhs, n0, n, start, stop):
            nc.tensor.matmul_mx(
                out=acc,
                lhsT=lhs[0][:, m0 : m0 + P].bitcast(FP8X4),
                lhsT_scale=lhs[1][:, m0 : m0 + P],
                rhs=rhs[0][:, n0 : n0 + n].bitcast(FP8X4),
                rhs_scale=rhs[1][:, n0 : n0 + n],
                start=start,
                stop=stop,
            )

        def cast_plain(copy, dst, src, i=4):
            copy(dst.rearrange("p (c i) j -> p c j i", i=i), src.rearrange("p j (c i) -> p c j i", i=i))

        EXPERT = {"e": 0, "f": 1, "s": E}
        MATRIX = {"1": w1, "3": w3}

        x_raw = [xraw.tile([P, J, T], F32, name=f"xr{s}") for s in range(PASSES)]
        w_raw = {}
        v_raw = {}
        codes = {}
        pairs = [[keep.tile([P, T, 2], BF16, name=f"pairs{s}{h}") for h in range(2)] for s in range(PASSES)]
        x4 = [group.tile([P, T, J], BF16, name=f"x4{s}", bufs=1, align_bytes=64) for s in range(PASSES)]
        g4 = [group.tile([P, E * C * J], BF16, name=f"g4{s}", bufs=1, align_bytes=64) for s in range(PASSES)]
        xs = [codes_of(T, f"xs{s}") for s in range(PASSES)]
        xg = [codes_of(E * C, f"xg{s}") for s in range(PASSES)]
        hidden = {"s": codes_of(T, "hs"), "e": codes_of(C, "he"), "f": codes_of(C, "hf")}

        def load_x(s, h):
            view = xT[s * 512 : (s + 1) * 512, :].rearrange("(p j) t -> p j t", j=J)
            nc.sync.dma_start(x_raw[s][:, 2 * h : 2 * h + 2, :], view[:, 2 * h : 2 * h + 2, :])

        def load_w(name, parts):
            w, e, s = MATRIX[name[1]], EXPERT[name[2]], int(name[3])
            wr = wraw.tile([P, J, H], F32, name="wr")
            view = w[e, s * 512 : (s + 1) * 512, :].rearrange("(p j) c -> p j c", j=J)
            step = H // parts
            for c in range(0, H, step):
                nc.sync.dma_start(wr[:, :, c : c + step], view[:, :, c : c + step])
            w_raw[name] = wr

        def load_v(name):
            vr = vraw.tile([P, J, N], F32, name="vr")
            nc.sync.dma_start(vr[:], w2[{"v0": 0, "v1": 1, "vs": E}[name]].rearrange("(p j) c -> p j c", j=J))
            v_raw[name] = vr

        def cast_pair(s, h, c, who):
            cast_plain(copiers[who], pairs[s][h][:], x_raw[s][:, 2 * h : 2 * h + 2, :])

        def cast_x(s, c, who):
            cast_plain(copiers[who], x4[s][:, c * XT : (c + 1) * XT, :], x_raw[s][:, :, c * XT : (c + 1) * XT])

        def gather(s, h):
            words = g4[s][:].bitcast(U32).rearrange("p (n h) -> p n h", h=2)
            window = pairs[s][h][:].rearrange("p t e -> p (t e)").bitcast(U32)
            nc.vector.tensor_copy(words[:, :, h], window.indirect(offsets[:]))

        def quantize_x(s):
            x4f = x4[s][:].rearrange("p t j -> p (t j)")
            quantize(xs[s], 0, x4f[:, :2048], 512)
            quantize(xs[s], 512, x4f[:, 2048:], 256)

        def quantize_g(s):
            quantize(xg[s], 0, g4[s][:], 512)

        grouped = {}

        def cast_w(name, who):
            g = group.tile([P, J * H], BF16, name="g", align_bytes=64)
            grouped[name] = g
            dst = g[:].rearrange("p (t m j) -> p m j t", t=J, j=J)
            src = w_raw[name][:].rearrange("p j (m t) -> p m j t", t=J)
            step = P // len(who)
            a = 0
            for w in sorted(set(who)):
                b = a + who.count(w) * step
                copiers[w](dst[:, a:b], src[:, a:b])
                a = b

        def quantize_w(name):
            codes[name] = codes_of(H, name)
            quantize(codes[name], 0, grouped[name][:], H)

        def cast_v(name, who):
            g = group.tile([P, N, J], BF16, name="gv", bufs=2, align_bytes=64)
            grouped[name] = g
            cast_plain(copiers[who], g[:], v_raw[name][:])

        def quantize_v(name):
            codes[name] = codes_of(N, name)
            quantize(codes[name], 0, grouped[name][:].rearrange("p n j -> p (n j)"), N)

        def product(w, e, i, name):
            x, col = (xs, i * TOK) if e == "s" else (xg, EXPERT[e] * C + i * TOK)
            acc = psum.tile([P, J, TOK], F32, name=name)
            for t in range(J):
                for s in range(PASSES):
                    mm(acc[:, t, :], codes[f"{w}{e}{s}"], t * P, x[s], col, TOK, s == 0, s == PASSES - 1)
            return acc

        silus = {}
        h2 = {}

        def front(e, i):
            a = product("w1", e, i, "a")
            sl = work.tile([P, TOK, J], F32, name="sl", bufs=6)
            nc.scalar.activation(sl[:], a[:].rearrange("p t n -> p n t"), SILU)
            silus[e, i] = sl

        def back(e, i, who="V"):
            b = product("w3", e, i, "b")
            if (e, i // 2) not in h2:
                hh = work.tile([P, 2, TOK, J], BF16, name="hh", align_bytes=64)
                h2[e, i // 2] = hh
            dst = h2[e, i // 2][:, i % 2]
            if who == "G":
                bc = work.tile([P, TOK, J], F32, name="bc", bufs=2)
                nc.scalar.copy(bc[:], b[:].rearrange("p t n -> p n t"))
                nc.gpsimd.tensor_tensor(dst, bc[:], silus[e, i][:], MULT)
            else:
                nc.vector.tensor_tensor(dst, b[:].rearrange("p t n -> p n t"), silus[e, i][:], MULT)

        def quantize_h(e, k):
            quantize(hidden[e], k * 2 * TOK, h2[e, k][:].rearrange("p c n t -> p (c n t)"), 2 * TOK)

        ys = [psum1.tile([P, 2, C], F32, name=f"ys{i}") for i in range(3)]
        weighted = {}

        def result(e):
            y = psum1.tile([P, 2, C], F32, name="y")
            yr = work.tile([P, 2, C], F32, name="yr", bufs=2)
            for r in range(2):
                mm(y[:, r, :], codes[{"e": "v0", "f": "v1"}[e]], r * P, hidden[e], 0, C, True, True)
            gate_e = gates[:, EXPERT[e] * C : (EXPERT[e] + 1) * C].rearrange("p (o c) -> p o c", o=1).to_broadcast([P, 2, C])
            nc.vector.tensor_tensor(yr[:], y[:], gate_e, MULT)
            weighted[e] = yr

        def scatter(e, r):
            cols = offsets[:, EXPERT[e] * C // 16 : (EXPERT[e] + 1) * C // 16]
            nc.vector.tensor_copy(routed[r][:].indirect(cols), weighted[e][:, r, :])

        def shared_sum():
            for r in range(2):
                mm(ys[r][:].rearrange("p a c -> p (a c)"), codes["vs"], r * P, hidden["s"], 0, 512, True, True)
            for r in range(2):
                mm(ys[2][:, r, :], codes["vs"], r * P, hidden["s"], 512, C, True, True)

        ysum = work.tile([P, T], F32, name="ysum", bufs=1)

        def shared_copy():
            nc.scalar.copy(ysum[:, :512], ys[0][:].rearrange("p a c -> p (a c)"))
            nc.scalar.copy(ysum[:, 512:], ys[2][:, 0, :])

        def finish(r, who):
            o = work.tile([P, T], F32, name="o", bufs=2)
            if who == "G":
                nc.gpsimd.tensor_tensor(o[:], routed[r][:], ysum[:], ADD)
            else:
                nc.vector.tensor_tensor(o[:, :512], ys[r][:].rearrange("p a c -> p (a c)"), routed[r][:, :512], ADD)
                nc.vector.tensor_tensor(o[:, 512:], ys[2][:, r, :], routed[r][:, 512:], ADD)
            nc.sync.dma_start(out[r * P : (r + 1) * P, :], o[:])

        nc.sync.dma_start(offsets[:], offs)
        load_x(0, 0)
        load_x(1, 0)
        load_x(1, 1)
        load_x(0, 1)
        load_w("w1s1", 1)
        load_w("w1s0", 1)
        load_w("w3s1", 1)
        load_w("w3s0", 1)
        load_w("w1e0", 1)
        load_w("w1e1", 1)
        load_w("w1f1", 1)
        load_w("w3e1", 1)
        load_v("v0")
        load_w("w3e0", 1)
        load_w("w1f0", 1)
        load_w("w3f0", 1)
        load_w("w3f1", 2)
        nc.sync.dma_start(gates[:], gate[0:P, :])
        load_v("vs")
        load_v("v1")
        cast_x(1, 0, "V")
        cast_pair(0, 1, 0, "V")
        cast_w("w1s1", "V")
        gather(0, 1)
        cast_pair(0, 0, 0, "V")
        cast_x(0, 0, "S")
        cast_w("w1s0", "S")
        cast_pair(1, 0, 0, "S")
        cast_x(0, 1, "S")
        quantize_w("w1s0")
        gather(1, 0)
        gather(0, 0)
        quantize_g(0)
        quantize_x(0)
        cast_w("w3s1", "S")
        quantize_w("w1s1")
        cast_x(1, 1, "S")
        cast_pair(1, 1, 0, "G")
        cast_w("w3s0", "V")
        quantize_x(1)
        cast_w("w1e0", "V")
        front("s", 1)
        cast_v("v0", "G")
        quantize_w("w3s1")
        gather(1, 1)
        front("s", 2)
        front("s", 0)
        quantize_w("w3s0")
        front("s", 5)
        back("s", 1)
        cast_w("w3e1", "SV")
        front("s", 4)
        quantize_g(1)
        quantize_w("w1e0")
        back("s", 5)
        back("s", 0)
        cast_w("w3e0", "V")
        cast_w("w1e1", "S")
        quantize_w("w3e1")
        back("s", 2)
        front("s", 3)
        quantize_w("w1e1")
        back("s", 4)
        quantize_h("s", 0)
        quantize_v("v0")
        cast_w("w1f1", "V")
        quantize_w("w3e0")
        cast_w("w1f0", "S")
        front("e", 0)
        back("s", 3)
        quantize_h("s", 2)
        back("e", 0)
        quantize_w("w1f1")
        quantize_h("s", 1)
        front("e", 1)
        back("e", 1)
        cast_w("w3f1", "S")
        cast_w("w3f0", "S")
        quantize_h("e", 0)
        quantize_w("w3f1")
        result("e")
        quantize_w("w1f0")
        quantize_w("w3f0")
        scatter("e", 0)
        front("f", 1)
        front("f", 0)
        back("f", 1)
        back("f", 0)
        cast_v("v1", "S")
        cast_v("vs", "S")
        quantize_v("v1")
        quantize_h("f", 0)
        quantize_v("vs")
        scatter("e", 1)
        shared_sum()
        shared_copy()
        result("f")
        scatter("f", 0)
        finish(0, "G")
        scatter("f", 1)
        finish(1, "V")
